import numpy as np
import ml_dtypes


def mxq(x, axis, fmt="e4m3"):
    dtype, down = {"e4m3": (ml_dtypes.float8_e4m3fn, 7), "e5m2": (ml_dtypes.float8_e5m2, 14)}[fmt]
    v = np.moveaxis(np.asarray(x, np.float32).astype(ml_dtypes.bfloat16).astype(np.float64), axis, -1)
    blocks = v.reshape(v.shape[:-1] + (-1, 32))
    amax = np.abs(blocks).max(-1, keepdims=True)
    byte = np.maximum(np.where(amax > 0, np.frexp(amax)[1] - 1 + 127, 0) - down, 1)
    scale = np.exp2(byte - 127.0)
    codes = (blocks / scale).astype(np.float32).astype(dtype).astype(np.float64)
    return np.moveaxis((codes * scale).reshape(v.shape), -1, axis)


WIDE = False


def mx_kscale(k):
    if not WIDE:
        return np.ones(k)
    levels = np.array([10, -10, 5, -5, 0])
    if k % 512:
        return np.exp2(np.random.permutation(np.resize(levels, k // 32))).repeat(32)
    a = np.empty((k // 512, 16))
    for p in range(k // 512):
        a[p, :8] = np.random.permutation(np.resize(levels, 8))
        for g in range(8):
            far = levels[np.abs(levels - a[p, g]) >= 10]
            a[p, g + 8] = far[np.random.randint(len(far))]
    return np.exp2(a.ravel()).repeat(32)


BF16 = ml_dtypes.bfloat16


def bf(x):
    return np.asarray(x, np.float32).astype(BF16)


def f64(x):
    return np.asarray(x).astype(np.float64)


E2M1 = np.array([0.0, 0.5, 1.0, 1.5, 2.0, 3.0, 4.0, 6.0, -0.0, -0.5, -1.0, -1.5, -2.0, -3.0, -4.0, -6.0])


def pack_weight(w, fmt):
    k, n = w.shape
    w = f64(bf(w)).reshape(k // 32, 32, n)
    amax = np.abs(w).max(1)
    if fmt == "e4m3":
        byte = np.frexp(amax)[1] - 1 + 127 - 7
    else:
        mant, ex = np.frexp(amax / 6.0)
        byte = np.where(mant > 0.5, ex, ex - 1) + 127
    byte = np.clip(np.where(amax > 0, byte, 1), 1, 254)
    scaled = (w * np.exp2(127.0 - byte)[:, None, :]).reshape(k, n).astype(np.float32)
    by_word = np.ascontiguousarray(scaled.reshape(k // 512, 128, 4, n).transpose(0, 1, 3, 2))
    if fmt == "e4m3":
        words = by_word.astype(ml_dtypes.float8_e4m3fn).view(np.uint8)
    else:
        c = by_word.astype(ml_dtypes.float4_e2m1fn).view(np.uint8) & 0xF
        words = c[..., 0::2] | (c[..., 1::2] << 4)
    return np.ascontiguousarray(words), np.ascontiguousarray(byte.astype(np.uint8).reshape(k // 512, 16, n))


def unpack_weight(words, scales, fmt):
    g, p, n, _ = words.shape
    if fmt == "e4m3":
        vals = np.ascontiguousarray(words).view(ml_dtypes.float8_e4m3fn).astype(np.float64)
    else:
        nib = np.empty((g, p, n, 4), np.uint8)
        nib[..., 0::2] = words & 0xF
        nib[..., 1::2] = words >> 4
        vals = E2M1[nib]
    vals = vals * np.repeat(np.exp2(scales.astype(np.float64) - 127.0), 8, axis=1)[..., None]
    return vals.transpose(0, 1, 3, 2).reshape(g * 512, n)
def pack4(w):
    words, scales = pack_weight(w, "e2m1")
    return words.reshape(words.shape[0], 128, -1), scales


def unpack4(words, scales):
    return unpack_weight(words.reshape(words.shape[0], 128, -1, 2), scales, "e2m1")


def planes(Y):
    n, m = Y.shape
    b = f64(bf(Y)).reshape(n // 32, 32, m)
    amax = np.abs(b).max(1)
    byte = np.clip(np.where(amax > 0, np.frexp(amax)[1] - 1 + 127 - 7, 1), 1, 254)
    codes = (b * np.exp2(127.0 - byte)[:, None, :]).reshape(n, m).astype(np.float32).astype(ml_dtypes.float8_e4m3fn).view(np.uint8)
    words = codes.reshape(n // 512, 128, 4, m).transpose(0, 1, 3, 2)
    return np.ascontiguousarray(words), np.ascontiguousarray(byte.astype(np.uint8).reshape(n // 512, 16, m))


B, N, M, D, E = 2, 1024, 1024, 512, 512


def scaled_correlation(faq, fbq):
    depth = faq.shape[-1]
    return (faq @ fbq.transpose(0, 2, 1)) / np.sqrt(depth)


def mutual_filter(c):
    ra = np.max(c, axis=2, keepdims=True)
    rb = np.max(c, axis=1, keepdims=True)
    return c * (c / ra) * (c / rb)


def setup_inputs():
    s = mx_kscale(D)
    t = mx_kscale(M)
    fa = bf(np.random.standard_normal((B, N, D)) * s)
    fb = bf(np.random.standard_normal((B, M, D)) / s)
    g = bf((1.0 + 0.1 * np.random.standard_normal(M)) * t)
    wt_words, wt_scales = pack4(2.0 * np.random.standard_normal((M, E)) / np.sqrt(M) / t[:, None])
    wr_words, wr_scales = pack4(0.5 * np.random.standard_normal((D, E)) / np.sqrt(D) / s[:, None])
    return {
        "fa": fa,
        "fb": fb,
        "g": g,
        "wt_words": wt_words,
        "wt_scales": wt_scales,
        "wr_words": wr_words,
        "wr_scales": wr_scales,
    }


def core(fa, fb, g, wt_words, wt_scales, wr_words, wr_scales):
    faq = mxq(f64(fa), 2, "e4m3")
    c = scaled_correlation(faq, mxq(f64(fb), 2, "e4m3"))
    f = mutual_filter(c)
    fg = f * f64(g)[None, None, :]
    t = mxq(fg, 2, "e4m3") @ unpack4(wt_words, wt_scales)
    r = faq @ unpack4(wr_words, wr_scales)
    return t + r


def reference(fa, fb, g, wt_words, wt_scales, wr_words, wr_scales):
    R_out = core(fa, fb, g, wt_words, wt_scales, wr_words, wr_scales)
    words, scales = planes(np.moveaxis(R_out, 1, 0).reshape(1024, -1))
    return R_out, words, scales

from contextlib import ExitStack

import concourse.mybir as mybir
from concourse.masks import make_identity

B, N, M, D, E = 2, 1024, 1024, 512, 512
FLOPS = B * (2 * N * M * D + 2 * N * M * E + 2 * N * D * E)

F32 = mybir.dt.float32
BF16 = mybir.dt.bfloat16
I32 = mybir.dt.int32
U32 = mybir.dt.uint32
U8 = mybir.dt.uint8
FP8X4 = mybir.dt.float8_e4m3fn_x4
FP4X4 = mybir.dt.float4_e2m1fn_x4
ALU = mybir.AluOpType
ACT = mybir.ActivationFunctionType
AX = mybir.AxisListType

P = 128
PACK = 4
GROUP = P * PACK
BANK = 512
TILES = N // P
INV_SQRT_D = 1.0 / D**0.5

AHEAD = 2
COL_COUNT = [4, 4, 4, 4, 3, 3, 2, 2, 2, 2, 2, 0, 0, 0, 0, 0]
FILT_COUNT = [0, 0, 0, 0, 1, 1, 2, 2, 2, 2, 2, 4, 3, 3, 2, 2]
PIECES = [2] * 12 + [1] * 10


def tile_mutualfiltercosttokenencoder_x2_kernel(
    tc, fa, fb, g, wt_words, wt_scales, wr_words, wr_scales, out_0, out_1, out_2
):
    nc = tc.nc
    with ExitStack() as ctx:
        keep = ctx.enter_context(tc.tile_pool(name="keep", bufs=1))
        work = ctx.enter_context(tc.tile_pool(name="work", bufs=3))
        psum = ctx.enter_context(tc.psum_pool(name="psum", bufs=1))
        ctx.enter_context(tc.manual_schedule())

        src = {"a": fa, "b": fb}
        raw = {}

        def load(x, b, grp, split):
            t = keep.tile([P, PACK, D], BF16, name="raw_%s%d%d" % (x, b, grp), align_bytes=64)
            rows = src[x][b, grp * GROUP : (grp + 1) * GROUP, :].rearrange("(p j) d -> p j d", j=PACK)
            step = PACK // split
            for s in range(0, PACK, step):
                nc.sync.dma_start(out=t[:, s : s + step, :], in_=rows[:, s : s + step, :])
            raw[(x, b, grp)] = t

        g_rows = keep.tile([P, 256], BF16, name="g_rows")
        w_scales = keep.tile([P, 3, E], U8, name="w_scales", align_bytes=64)
        w_words = keep.tile([P, 3, 2 * E], U8, name="w_words", align_bytes=64)
        ident = keep.tile([P, P], F32, name="ident")
        warm = keep.tile([P, 1], F32, name="warm")

        load("b", 0, 0, 2)
        load("a", 0, 0, 2)
        make_identity(nc, ident[:])
        nc.vector.memset(g_rows[:], 0.0)
        nc.vector.memset(w_scales[:].rearrange("p s e -> p (s e)").bitcast(I32), 0)
        nc.scalar.activation(out=warm[:], in_=ident[:, 0:1], func=ACT.Square)
        load("b", 0, 1, 2)
        nc.sync.dma_start(out=g_rows[0:4, :], in_=g.rearrange("(r x) -> r x", r=4))
        load("a", 0, 1, 1)
        for x, grp in (("b", 0), ("a", 0), ("b", 1), ("a", 1)):
            load(x, 1, grp, 1)
        nc.sync.dma_start(out=w_words[:, 0, :].bitcast(I32), in_=wr_words[0].bitcast(I32))
        nc.sync.dma_start(
            out=w_words[:, 1:3, :].bitcast(I32), in_=wt_words.rearrange("s p c -> p s c").bitcast(I32)
        )
        for q in range(4):
            nc.sync.dma_start(
                out=w_scales[32 * q : 32 * q + 4, 0, :].bitcast(I32),
                in_=wr_scales[0, 4 * q : 4 * q + 4, :].bitcast(I32),
            )
            nc.sync.dma_start(
                out=w_scales[32 * q : 32 * q + 4, 1:3, :].bitcast(I32),
                in_=wt_scales[:, 4 * q : 4 * q + 4, :].rearrange("s r e -> r s e").bitcast(I32),
            )

        codes = {}
        scales = {}
        for x in ("a", "b"):
            for b in range(B):
                codes[(x, b)] = keep.tile([P, N], U32, name="codes_%s%d" % (x, b), align_bytes=64)
                scales[(x, b)] = keep.tile([P, N], U8, name="scales_%s%d" % (x, b), align_bytes=64)

        row_max0 = keep.tile([P, B * TILES], F32, name="row_max0")
        row_max = keep.tile([P, B * TILES], F32, name="row_max")
        row_inv = keep.tile([P, B * TILES], F32, name="row_inv")
        col_part = keep.tile([P, B * TILES, 2], F32, name="col_part")
        col_max = keep.tile([P, B * TILES], F32, name="col_max")
        col_inv = keep.tile([P, B * TILES], F32, name="col_inv")
        col_gain = keep.tile([P, B * TILES], F32, name="col_gain")
        g_cols = keep.tile([P, TILES], F32, name="g_cols")
        out_scales = keep.tile([P, 2, B * E], U8, name="out_scales", align_bytes=64)

        grouped = {}
        turn_bank = {}
        free_banks = ["bank%d" % n for n in range(8)]
        bank_of = {}

        def take_bank(key, shape):
            bank_of[key] = free_banks.pop(0)
            return psum.tile(shape, F32, name="bank", tag=bank_of[key])

        def give_bank(key):
            free_banks.append(bank_of[key])

        def copy(engine, out, in_):
            if engine == "act":
                nc.scalar.copy(out=out, in_=in_)
            elif engine == "pool":
                nc.gpsimd.tensor_scalar(out=out, in0=in_, scalar1=1.0, scalar2=0.0, op0=ALU.mult, op1=ALU.add)
            else:
                nc.vector.tensor_copy(out=out, in_=in_)

        def in_turn(x, b, grp, half):
            bank = take_bank((x, b, grp, half), [P, 2, 2, P])
            words = raw[(x, b, grp)][:].bitcast(F32)
            for s in range(2):
                for v in range(2):
                    nc.tensor.transpose(bank[:, s, v, :], words[:, 2 * half + s, v : 256 : 2], ident[:])
            turn_bank[(x, b, grp, half)] = bank

        def in_evac(x, b, grp, half, engine):
            if half == 0:
                grouped[(x, b, grp)] = work.tile([P, 2, 1024], BF16, name="grouped", tag="grouped", align_bytes=64)
            bank = turn_bank[(x, b, grp, half)]
            dst = grouped[(x, b, grp)][:, half, :].bitcast(F32)
            if x == "a":
                copy(engine, dst.rearrange("p (s r v) -> p s r v", s=2, v=2), bank[:].rearrange("p s v r -> p s r v"))
            else:
                copy(engine, dst.rearrange("p (r s v) -> p r s v", s=2, v=2), bank[:].rearrange("p s v r -> p r s v"))
            give_bank((x, b, grp, half))

        def in_quant(x, b, grp, h0, h1):
            cols = slice(grp * GROUP + 256 * h0, grp * GROUP + 256 * h1)
            nc.vector.quantize_mx(
                out=codes[(x, b)][:, cols].bitcast(FP8X4),
                scales=scales[(x, b)][:, cols],
                in_=grouped[(x, b, grp)][:, h0:h1, :].rearrange("p h c -> p (h c)"),
            )

        g_perm = keep.tile([P, 2, P], F32, name="g_perm")

        def gain_permute():
            nc.scalar.copy(
                out=g_perm[:].rearrange("p u (q e) -> p u q e", e=2),
                in_=g_rows[:].rearrange("p (q u e) -> p u q e", u=2, e=2),
            )

        def gain_setup():
            bank = take_bank("g", [P, 2, 2, P])
            for u in range(2):
                nc.tensor.transpose(bank[:, 0, u, :], g_perm[:, u, :], ident[:])
            nc.scalar.activation(
                out=g_cols[:].rearrange("p (grp u hh) -> p grp u hh", u=2, hh=2),
                in_=bank[:, 0, :, 0:4].rearrange("p u (grp hh) -> p grp u hh", hh=2),
                func=ACT.Copy,
                scale=INV_SQRT_D,
            )
            give_bank("g")

        c_bank = {}
        c_copy = {}
        cube = {}

        def corr(unit):
            kind, i, h = unit
            b, j = divmod(i, TILES)
            stat, mov = ("a", "b") if kind == "row" else ("b", "a")
            bank = take_bank(unit, [P, BANK])
            sc = slice(j * P, (j + 1) * P)
            mc = slice(h * BANK, (h + 1) * BANK)
            nc.tensor.matmul_mx(
                out=bank[:],
                lhsT=codes[(stat, b)][:, sc].bitcast(FP8X4),
                lhsT_scale=scales[(stat, b)][:, sc],
                rhs=codes[(mov, b)][:, mc].bitcast(FP8X4),
                rhs_scale=scales[(mov, b)][:, mc],
                start=True,
                stop=True,
            )
            c_bank[unit] = bank

        def take_max(unit):
            kind, i, h = unit
            bank = c_bank[unit]
            if kind == "col":
                nc.vector.tensor_reduce(out=col_part[:, i, h : h + 1], in_=bank[:], axis=AX.X, op=ALU.max)
            else:
                if h == 0:
                    c_copy[i] = work.tile([P, M], F32, name="c_copy", tag="c_copy")
                nc.vector.tensor_scalar(
                    out=c_copy[i][:, h * BANK : (h + 1) * BANK],
                    in0=bank[:],
                    scalar1=1.0,
                    scalar2=None if h == 0 else row_max0[:, i : i + 1],
                    op0=ALU.mult,
                    op1=ALU.max,
                    accum_out=(row_max0 if h == 0 else row_max)[:, i : i + 1],
                )
            give_bank(unit)

        def row_recip(i):
            nc.vector.reciprocal(out=row_inv[:, i : i + 1], in_=row_max[:, i : i + 1])

        def make_cube(i):
            sq = work.tile([P, M], F32, name="sq", tag="sq")
            nc.scalar.activation(out=sq[:], in_=c_copy[i][:], func=ACT.Square, scale=row_inv[:, i : i + 1])
            cube[i] = work.tile([P, M], F32, name="cube", tag="cube", bufs=7)
            nc.gpsimd.tensor_tensor(out=cube[i][:], in0=c_copy[i][:], in1=sq[:], op=ALU.mult)

        def col_cols(b, h):
            return slice(b * TILES + 4 * h, b * TILES + 4 * h + 4)

        def col_finish(b, h, step):
            cols = col_cols(b, h)
            if step == 0:
                nc.vector.tensor_reduce(out=col_max[:, cols], in_=col_part[:, cols, :], axis=AX.X, op=ALU.max)
            elif step == 1:
                nc.vector.reciprocal(out=col_inv[:, cols], in_=col_max[:, cols])
            else:
                nc.vector.tensor_tensor(
                    out=col_gain[:, cols], in0=col_inv[:, cols], in1=g_cols[:, 4 * h : 4 * h + 4], op=ALU.mult
                )

        gain_bank = {}

        def spread_gain(b, h):
            bank = take_bank(("gain", b, h), [P, 4, P])
            for j in range(4):
                col = b * TILES + 4 * h + j
                nc.tensor.transpose(bank[:, j, :], col_gain[:, col : col + 1].to_broadcast([P, P]), ident[:])
            gain_bank[(b, h)] = bank

        fg = {}
        fg_grouped = {}
        fg_codes = {}
        fg_scales = {}
        out_bank = {}
        out_sb = {}
        out_bf = {}

        def filt(i, h):
            if h == 0:
                fg[i] = work.tile([P, M], BF16, name="fg", tag="fg", align_bytes=64)
            nc.vector.scalar_tensor_tensor(
                out=fg[i][:, h * BANK : (h + 1) * BANK],
                in0=cube[i][:, h * BANK : (h + 1) * BANK],
                scalar=row_max[:, i : i + 1],
                in1=gain_bank[(i // TILES, h)][:].rearrange("p j q -> p (j q)"),
                op0=ALU.mult,
                op1=ALU.mult,
            )
            if i % TILES == TILES - 1:
                give_bank(("gain", i // TILES, h))

        def fg_turn(i):
            bank = take_bank(("turn", i), [P, 2, 2, P])
            words = fg[i][:].bitcast(F32)
            for s in range(2):
                for u in range(2):
                    w0 = (2 * s + u) * P
                    nc.tensor.transpose(bank[:, s, u, :], words[:, w0 : w0 + P], ident[:])
            turn_bank[i] = bank

        def fg_evac(i, engine):
            fg_grouped[i] = work.tile([P, M], BF16, name="fg_grouped", tag="fg_grouped", align_bytes=64)
            copy(
                engine,
                fg_grouped[i][:].bitcast(F32).rearrange("p (s n u) -> p s n u", s=2, u=2),
                turn_bank[i][:].rearrange("p s u n -> p s n u"),
            )
            give_bank(("turn", i))

        def fg_quant(i):
            fg_codes[i] = work.tile([P, 2 * P], U32, name="fg_codes", tag="fg_codes", align_bytes=64)
            fg_scales[i] = work.tile([P, 2 * P], U8, name="fg_scales", tag="fg_scales", align_bytes=64)
            nc.vector.quantize_mx(out=fg_codes[i][:].bitcast(FP8X4), scales=fg_scales[i][:], in_=fg_grouped[i][:])

        def out_mm(i):
            b, j = divmod(i, TILES)
            bank = take_bank(("out", i), [P, E])
            sc = slice(j * P, (j + 1) * P)
            for s in range(3):
                if s == 0:
                    lhs, lhs_scale = codes[("a", b)][:, sc], scales[("a", b)][:, sc]
                else:
                    cols = slice((s - 1) * P, s * P)
                    lhs, lhs_scale = fg_codes[i][:, cols], fg_scales[i][:, cols]
                nc.tensor.matmul_mx(
                    out=bank[:],
                    lhsT=lhs.bitcast(FP8X4),
                    lhsT_scale=lhs_scale,
                    rhs=w_words[:, s, :].bitcast(FP4X4),
                    rhs_scale=w_scales[:, s, :],
                    start=(s == 0),
                    stop=(s == 2),
                )
            out_bank[i] = bank

        def out_evac(i, engine):
            quad, t = divmod(i, PACK)
            b, grp = divmod(quad, 2)
            if t == 0:
                out_sb[quad] = work.tile([P, PACK, E], F32, name="out_sb", tag="out_sb", bufs=2)
            copy(engine, out_sb[quad][:, t, :], out_bank[i][:])
            give_bank(("out", i))
            rows = out_0[b, grp * GROUP : (grp + 1) * GROUP, :].rearrange("(p t) e -> p t e", t=PACK)
            nc.sync.dma_start(out=rows[:, t, :], in_=out_sb[quad][:, t, :])

        def out_group(quad, e0, e1, engine):
            if e0 == 0:
                out_bf[quad] = work.tile([P, E, PACK], BF16, name="out_bf", tag="out_bf", bufs=2, align_bytes=64)
            cols = slice(e0, e1)
            copy(engine, out_bf[quad][:, cols, :], out_sb[quad][:, :, cols].rearrange("p t e -> p e t"))

        def out_quant(quad):
            b, grp = divmod(quad, 2)
            words = work.tile([P, E], U32, name="out_words", tag="out_words", bufs=2, align_bytes=64)
            nc.vector.quantize_mx(
                out=words[:].bitcast(FP8X4),
                scales=out_scales[:, grp, b * E : (b + 1) * E],
                in_=out_bf[quad][:].rearrange("p e t -> p (e t)"),
            )
            dst = out_1[grp].rearrange("p m t -> p (m t)").bitcast(I32)
            nc.sync.dma_start(out=dst[:, b * E : (b + 1) * E], in_=words[:].bitcast(I32))

        def store_scales():
            for q in range(4):
                eng = nc.sync if q % 2 == 0 else nc.scalar
                eng.dma_start(
                    out=out_2[:, 4 * q : 4 * q + 4, :].rearrange("s r m -> r s m").bitcast(I32),
                    in_=out_scales[32 * q : 32 * q + 4, :, :].bitcast(I32),
                )

        col0 = [("col", j, 0) for j in range(8)] + [("col", j, 1) for j in range(8)]
        col1 = [("col", TILES + j, h) for jj in (0, 4) for h in (0, 1) for j in range(jj, jj + 4)]
        cols = col0 + col1
        halves = [("filt", i, h) for i in range(16) for h in range(2)]
        halves[13], halves[14] = halves[14], halves[13]
        cols_in = {}
        filt_in = {}
        for k in range(16):
            cols_in[k] = cols[sum(COL_COUNT[:k]) : sum(COL_COUNT[: k + 1])]
            filt_in[k] = halves[sum(FILT_COUNT[:k]) : sum(FILT_COUNT[: k + 1])]
        rest = halves[sum(FILT_COUNT) :]
        prep_in = {1: ("b", 0), 2: ("a", 0), 3: ("a", 1), 4: ("b", 1)}
        finish_in = {2: (0, 0), 3: (0, 1), 7: (1, 0), 10: (1, 1)}

        units = []
        for k in range(16):
            cu = cols_in.get(k, [])
            if k == 0:
                units += [("row", 0, 0)] + cu[:2] + [("row", 0, 1)] + cu[2:]
            else:
                units += [("row", k, 0)] + cu[:1] + [("row", k, 1)] + cu[1:]
        issued = [0]

        def run(item):
            if item[0] == "filt":
                filt(item[1], item[2])
                return
            pos = units.index(item)
            while issued[0] <= min(pos + AHEAD, len(units) - 1):
                corr(units[issued[0]])
                issued[0] += 1
            take_max(item)

        in_turn("b", 0, 0, 0)
        in_turn("b", 0, 0, 1)
        in_turn("a", 0, 0, 0)
        in_turn("a", 0, 0, 1)
        in_evac("b", 0, 0, 0, "act")
        in_evac("b", 0, 0, 1, "dve")
        in_evac("a", 0, 0, 0, "act")
        in_quant("b", 0, 0, 0, 2)
        in_evac("a", 0, 0, 1, "act")
        in_quant("a", 0, 0, 0, 1)
        in_turn("b", 0, 1, 0)
        in_turn("b", 0, 1, 1)
        in_quant("a", 0, 0, 1, 2)
        in_evac("b", 0, 1, 0, "act")
        in_evac("b", 0, 1, 1, "act")
        run(units[0])
        in_turn("a", 0, 1, 0)
        in_turn("a", 0, 1, 1)
        in_quant("b", 0, 1, 0, 2)
        gain_permute()
        in_evac("a", 0, 1, 0, "act")
        in_evac("a", 0, 1, 1, "act")
        run(units[1])
        run(units[2])
        run(units[3])
        run(units[4])
        row_recip(0)
        make_cube(0)
        in_quant("a", 0, 1, 0, 2)
        run(units[5])
        gain_setup()

        filtered = []
        evacuated = []
        pieces = []
        to_quant = []
        for k in range(1, 16):
            cu = cols_in.get(k, [])
            xs = cu + filt_in[k]
            turning = list(filtered)
            filtered = []
            quanting = list(evacuated)
            evacuated = []
            if k < 16:
                run(("row", k, 0))
            if k in prep_in:
                in_turn(prep_in[k][0], 1, prep_in[k][1], 0)
            for i in turning:
                fg_turn(i)
            for x in xs[:1]:
                run(x)
            if k < 16:
                run(("row", k, 1))
            if k in prep_in:
                in_turn(prep_in[k][0], 1, prep_in[k][1], 1)
            for x in xs[1:2]:
                run(x)
            if k - 1 in finish_in:
                col_finish(finish_in[k - 1][0], finish_in[k - 1][1], 0)
            if k < 16:
                row_recip(k)
                make_cube(k)
            if k - 1 in finish_in:
                col_finish(finish_in[k - 1][0], finish_in[k - 1][1], 1)
            if k in prep_in:
                in_evac(prep_in[k][0], 1, prep_in[k][1], 0, "act")
                in_evac(prep_in[k][0], 1, prep_in[k][1], 1, "act")
            for i in turning:
                fg_evac(i, "act")
                evacuated.append(i)
            for i in quanting:
                fg_quant(i)
            if k - 1 in finish_in:
                col_finish(finish_in[k - 1][0], finish_in[k - 1][1], 2)
            if k - 1 in prep_in:
                in_quant(prep_in[k - 1][0], 1, prep_in[k - 1][1], 0, 2)
            for quad in to_quant:
                out_quant(quad)
            to_quant = []
            if k - 1 in finish_in and k < TILES:
                spread_gain(finish_in[k - 1][0], finish_in[k - 1][1])
            ready = list(pieces)
            for i in quanting:
                out_mm(i)
                out_evac(i, "act")
                if i % PACK == PACK - 1:
                    pieces.extend([(i // PACK, e0) for e0 in range(0, E, P)])
            for quad, e0 in ready[: PIECES[k]]:
                pieces.remove((quad, e0))
                out_group(quad, e0, e0 + P, "act")
                if e0 == E - P:
                    to_quant.append(quad)
            if ("filt", 7, 0) in xs:
                spread_gain(1, 0)
            for x in xs[2:]:
                run(x)
            if ("filt", 7, 1) in xs:
                spread_gain(1, 1)
            for x in xs:
                if x[0] == "filt" and x[2] == 1:
                    filtered.append(x[1])
        assert filtered == [12] and evacuated == [11] and rest[0] == ("filt", 13, 0), (filtered, evacuated, rest, pieces, to_quant)
        assert to_quant == [] and pieces == [(1, 256), (1, 384)], (pieces, to_quant)
        fg_turn(12)
        filt(13, 0)
        fg_evac(12, "dve")
        filt(13, 1)
        fg_turn(13)
        out_group(1, 256, 512, "act")
        filt(14, 0)
        fg_evac(13, "dve")
        filt(14, 1)
        fg_turn(14)
        fg_evac(14, "act")
        fg_quant(11)
        fg_quant(12)
        out_mm(11)
        out_mm(12)
        fg_quant(13)
        out_evac(11, "act")
        out_quant(1)
        filt(15, 0)
        filt(15, 1)
        out_mm(13)
        fg_turn(15)
        out_evac(12, "act")
        fg_quant(14)
        out_group(2, 0, 256, "pool")
        fg_evac(15, "dve")
        out_mm(14)
        out_evac(13, "act")
        out_group(2, 256, 512, "act")
        fg_quant(15)
        out_mm(15)
        out_evac(14, "dve")
        out_quant(2)
        out_evac(15, "dve")
        out_group(3, 0, 160, "act")
        out_group(3, 160, 512, "dve")
        out_quant(3)
        store_scales()
